import numpy as np, ml_dtypes
CORES = [169,41,209,81,249,121]
N = 6
MB, TK = 8, 128
def setup_inputs(rng):
    return {"x": rng.standard_normal((N, MB, 128, TK), dtype=np.float32).astype(ml_dtypes.bfloat16), "w": (rng.standard_normal((N, 128, 128), dtype=np.float32) / 8).astype(ml_dtypes.bfloat16), "u": (rng.standard_normal((N, 128, 128), dtype=np.float32) / 8).astype(ml_dtypes.bfloat16)}
def reference(x, w, u):
    def run(a, W, order):
        for s in order:
            a = np.maximum(np.einsum("kf,bkn->bfn", W[s].astype(np.float64), a), 0.0)
        return a
    dt = ml_dtypes.bfloat16 if x.dtype != np.float64 else np.float64
    y = np.full(x.shape, np.nan, dt)
    z = np.full(x.shape, np.nan, dt)
    y[N - 1] = run(x[0].astype(np.float64), w, range(N)).astype(dt)
    z[0] = run(x[N - 1].astype(np.float64), u, range(N - 1, -1, -1)).astype(dt)
    return {"y": y, "z": z}

@@ -1,0 +1,288 @@
+from concourse.bass import DstId, RemoteDMATransfer
+from concourse.mybir import AluOpType
+
+NL, MB, TK = 6, 8, 128
+UNITS = [(0, 2, 1, 0), (2, 2, 1, 0), (4, 2, 2, 0), (6, 2, 2, 0)]
+SUB = 2
+LEAD = 2
+GRP = 2
+NU = len(UNITS)
+KMAX = max(u[2] for u in UNITS)
+
+SCRATCH = {
+    "xs": ("sbuf", [128, MB * TK], "bfloat16"),
+    "rin": ("sbuf", [128, MB * TK], "bfloat16"),
+    "wb": ("sbuf", [128, 2 * NL * 128], "bfloat16"),
+    "zero": ("sbuf", [128, SUB * TK], "float32"),
+    "wst": ("dram", [2, 128, 128], "bfloat16"),
+}
+for _j in range(NL):
+    SCRATCH["a%d" % _j] = ("sbuf", [128, MB * TK], "bfloat16")
+for _b in range(8):
+    SCRATCH["ps%d" % _b] = ("psum", [128, 512], "float32")
+
+SEMAPHORES = (["pe", "dv", "zs", "sent", "sq0", "sq1", "stg0", "stg1", "rl0", "rl1"]
+              + ["ws%d" % s for s in range(2 * NL)] + ["lx%d" % m for m in range(MB)]
+              + ["ar%d" % c for c in range(NU)] + ["fn%d" % c for c in range(NU)])
+
+
+def _engines(mask):
+    return [b for b in range(mask.bit_length()) if (mask >> b) & 1]
+
+
+def _count(mask):
+    return len(_engines(mask))
+
+
+def _part(mask, parts, k):
+    e = _engines(mask)
+    n = len(e) // parts
+    return sum(1 << b for b in e[k * n:(k + 1) * n])
+
+
+def _pow2(n):
+    p = 1
+    while p < n:
+        p *= 2
+    return p
+
+
+def _uniq(seq):
+    out = []
+    for v in seq:
+        if v not in out:
+            out.append(v)
+    return out
+
+
+def _pieces(u):
+    m0, nm = UNITS[u][0], UNITS[u][1]
+    return [(m, min(SUB, m0 + nm - m)) for m in range(m0, m0 + nm, SUB)]
+
+
+def _plan(T, topo):
+    cores = list(T.cores)
+    world = range(2 * topo.CORES_PER_HOST)
+
+    def neighbours(c):
+        n = [d for d in world if d not in cores and topo.host(d) == topo.host(c) and topo.chip(d) == topo.chip(c)]
+        return [d for d in n if topo.die(d) == topo.die(c)], [d for d in n if topo.die(d) != topo.die(c)]
+
+    S = []
+    for st in range(2):
+        line = cores if st == 0 else cores[::-1]
+        same, other = neighbours(line[-1])
+        near = same + other
+        S.append({"line": line, "src": line[0], "dst": line[-1],
+                  "work": [line[-1] if u[3] == 0 else near[u[3] - 1] for u in UNITS]})
+    local, direct, hand, relay, wexp = {}, {}, {}, {}, {}
+    for h in cores:
+        hops = []
+        for st in range(2):
+            j = S[st]["line"].index(h)
+            want = []
+            if j < KMAX:
+                want.append((j - 0.5, S[st]["src"]))
+            for u in range(NU):
+                e = (j + (0.25 if UNITS[u][3] else 0), S[st]["work"][u])
+                if j >= UNITS[u][2] and e not in want:
+                    want.append(e)
+            for pr, d in want:
+                if d == h:
+                    local.setdefault(h, []).append((pr, j, st))
+                    wexp[(d, st, j)] = 16
+                elif topo.may_write(h, d):
+                    direct.setdefault(h, []).append((pr, j, st, d))
+                    wexp[(d, st, j)] = _count(topo.mask(h, d))
+                else:
+                    hops.append((pr, j, st, d))
+        if hops:
+            same, other = neighbours(h)
+            same = [c for c in same if all(topo.may_write(c, e[3]) for e in hops)]
+            other = [c for c in other if all(topo.may_write(c, e[3]) for e in hops)]
+            ring = []
+            for i in range(max(len(same), len(other))):
+                ring += other[i:i + 1] + same[i:i + 1]
+            for i, (pr, j, st, d) in enumerate(sorted(hops)):
+                r = ring[i % len(ring)]
+                relay.setdefault(r, []).append((pr, j, st, d))
+                wexp[(d, st, j)] = _count(topo.mask(r, d))
+                if (r, st) not in hand.setdefault(h, []):
+                    hand[h].append((r, st))
+    return {"S": S, "local": local, "direct": direct, "hand": hand, "relay": relay, "wexp": wexp}
+
+
+def _in_order(us):
+    seq = [(UNITS[u][2], u, p) for u in us[:LEAD] for p in _pieces(u)]
+    for g0 in range(0, len(us), GRP):
+        for j in range(NL):
+            for u in us[g0:g0 + GRP]:
+                for p in _pieces(u):
+                    if j >= UNITS[u][2] and (j, u, p) not in seq:
+                        seq.append((j, u, p))
+    return seq
+
+
+def rank_program(g, core, T, topo):
+    P = _plan(T, topo)
+    S, sem = P["S"], T.sem
+    sent = [0]
+    queues = [g.sync, g.scalar]
+    nq = [0]
+    stores = [0, 0]
+    last = T["a%d" % (NL - 1)]
+
+    def slot(st, j):
+        return T.wb[:, (st * NL + j) * 128:(st * NL + j + 1) * 128]
+
+    def wsem(st, j):
+        return sem["ws%d" % (st * NL + j)]
+
+    def ucols(u):
+        return UNITS[u][0] * TK, (UNITS[u][0] + UNITS[u][1]) * TK
+
+    def load(out, in_, s):
+        queues[nq[0] % 2].dma_start(out, in_).then_inc(s, 16)
+        nq[0] += 1
+
+    def write(d, out, in_, rsem):
+        rid, pid = topo.addr(d, core)
+        m = topo.mask(core, d)
+        g.remote_dma(out_ap=out, in_ap=in_, remote_sem=rsem, local_sem=sem.sent, pid=pid, routing_id=rid,
+                     dma_engine_mask=m)
+        sent[0] += _count(m)
+
+    outs = [st for st in range(2) if S[st]["src"] == core]
+    ins = [st for st in range(2) if core in S[st]["work"] or core == S[st]["dst"]]
+    so = outs[0] if outs else None
+    si = ins[0] if ins else None
+    wt = [T.w, T.u] if T.rank_of(core) is not None else None
+
+    mine_local = sorted(P["local"].get(core, []))
+    staged = _uniq([e[2] for e in sorted(P["direct"].get(core, []))] + [st for _, st in P["hand"].get(core, [])])
+    if not outs:
+        for st in staged:
+            load(T.wst[st], wt[st][:], sem["stg%d" % st])
+    for pr, j, st in mine_local:
+        if st == so:
+            load(slot(st, j), wt[st][:], wsem(st, j))
+    if outs:
+        for m in range(MB):
+            load(T.xs[:, m * TK:(m + 1) * TK], T.x[m], sem["lx%d" % m])
+    for pr, j, st in mine_local:
+        if st != so:
+            load(slot(st, j), wt[st][:], wsem(st, j))
+    if outs:
+        for st in staged:
+            load(T.wst[st], wt[st][:], sem["stg%d" % st])
+
+    tasks = []
+    if outs:
+        tasks += [(so, j, u, p) for u in range(NU) for j in range(UNITS[u][2]) for p in _pieces(u)]
+    mine = [u for u in range(NU) if ins and S[si]["work"][u] == core]
+    tasks += [(si,) + t for t in _in_order(mine)]
+    idx = {t: i for i, t in enumerate(tasks)}
+
+    have, dv_seen = [], 0
+    for i, (st, j, u, (m0, nm)) in enumerate(tasks):
+        lo, hi = m0 * TK, (m0 + nm) * TK
+        if (st, j) not in have:
+            g.tensor.wait_ge(wsem(st, j), P["wexp"][(core, st, j)])
+            have.append((st, j))
+        need = i - 7
+        if j == 0:
+            for m in range(m0, m0 + nm):
+                g.tensor.wait_ge(sem["lx%d" % m], 16)
+            a = T.xs
+        elif st == si and j == UNITS[u][2]:
+            if ("ar", u) not in have:
+                g.tensor.wait_ge(sem["ar%d" % u], _count(topo.mask(S[si]["src"], core)))
+                have.append(("ar", u))
+            a = T.rin
+        else:
+            need = max(need, idx[(st, j - 1, u, (m0, nm))] + 1)
+            a = T["a%d" % (j - 1)]
+        if need > dv_seen:
+            g.tensor.wait_ge(sem.dv, need)
+            dv_seen = need
+        g.tensor.matmul(T["ps%d" % (i % 8)][:, 0:hi - lo], slot(st, j), a[:, lo:hi], start=True, stop=True).then_inc(sem.pe, 1)
+    if tasks:
+        g.vector.memset(T.zero[:], 0.0).then_inc(sem.zs, 1)
+        g.vector.wait_ge(sem.zs, 1)
+    for i, (st, j, u, (m0, nm)) in enumerate(tasks):
+        lo, hi = m0 * TK, (m0 + nm) * TK
+        g.vector.wait_ge(sem.pe, i + 1)
+        g.vector.tensor_tensor(out=T["a%d" % j][:, lo:hi], in0=T["ps%d" % (i % 8)][:, 0:hi - lo],
+                               in1=T.zero[:, 0:hi - lo], op=AluOpType.max).then_inc(sem.dv, 1)
+
+    def done(st, j, u):
+        return max(idx[(st, j, u, p)] for p in _pieces(u)) + 1
+
+    def send_weights():
+        got = []
+        for pr, j, st, d in sorted(P["direct"].get(core, [])):
+            if st not in got:
+                g.wait_ge(sem["stg%d" % st], 16)
+                got.append(st)
+            write(d, slot(st, j), T.wst[st], wsem(st, j))
+        hand = P["hand"].get(core, [])
+        if hand:
+            for st in _uniq([st for _, st in hand]):
+                if st not in got:
+                    g.wait_ge(sem["stg%d" % st], 16)
+                    got.append(st)
+            trs = []
+            for k, (r, st) in enumerate(hand):
+                rid, pid = topo.addr(r, core)
+                m = _part(topo.mask(core, r), _pow2(len(hand)), k)
+                trs.append(RemoteDMATransfer(dst_ids=[DstId(rid=rid, pnc=pid)], dma_engine_mask=m,
+                                             remote_sem=sem["rl%d" % st], src=T.wst[st], dst=T.wst[st]))
+                sent[0] += _count(m)
+            g.remote_dma_fused(trs, local_sem=sem.sent)
+
+    if not outs:
+        send_weights()
+    else:
+        for u in range(NU):
+            lo, hi = ucols(u)
+            k = UNITS[u][2]
+            g.wait_ge(sem.dv, done(so, k - 1, u))
+            write(S[so]["work"][u], T.rin[:, lo:hi], T["a%d" % (k - 1)][:, lo:hi], sem["ar%d" % u])
+        send_weights()
+    if core in P["relay"]:
+        jobs = sorted(P["relay"][core])
+        holder = [h for h in P["hand"] if (core, jobs[0][2]) in P["hand"][h]][0]
+        n_in = _count(_part(topo.mask(holder, core), _pow2(len(P["hand"][holder])), 0))
+        got = []
+        for pr, j, st, d in jobs:
+            if st not in got:
+                g.wait_ge(sem["rl%d" % st], n_in)
+                got.append(st)
+            write(d, slot(st, j), T.wst[st], wsem(st, j))
+    if ins and core != S[si]["dst"]:
+        for u in mine:
+            lo, hi = ucols(u)
+            g.wait_ge(sem.dv, done(si, NL - 1, u))
+            write(S[si]["dst"], last[:, lo:hi], last[:, lo:hi], sem["fn%d" % u])
+
+    if ins and core == S[si]["dst"]:
+        res = T.y if si == 0 else T.z
+        jobs = [(idx[t] + 1, t[2], m) for t in tasks if t[0] == si and t[1] == NL - 1 for m in range(t[3][0], t[3][0] + t[3][1])]
+        jobs += [(None, u, m) for u in range(NU) if u not in mine for m in range(UNITS[u][0], UNITS[u][0] + UNITS[u][1])]
+        for v, u, m in jobs:
+            q = nq[0] % 2
+            nq[0] += 1
+            if v is not None:
+                queues[q].wait_ge(sem.dv, v)
+            else:
+                queues[q].wait_ge(sem["fn%d" % u], _count(topo.mask(S[si]["work"][u], core)))
+            queues[q].dma_start(res[m], last[:, m * TK:(m + 1) * TK]).then_inc(sem["sq%d" % q], 16)
+            stores[q] += 16
+        for q in range(2):
+            if stores[q]:
+                queues[q].wait_ge(sem["sq%d" % q], stores[q])
+
+    if tasks:
+        g.wait_ge(sem.dv, len(tasks))
+    if sent[0]:
+        g.wait_ge(sem.sent, sent[0])

@@ -2,10 +2,8 @@ from concourse.bass import DstId, RemoteDMATransfer
 from concourse.mybir import AluOpType
 
 NL, MB, TK = 6, 8, 128
-UNITS = [(0, 2, 1, 0), (2, 2, 1, 0), (4, 2, 2, 0), (6, 2, 2, 0)]
-SUB = 2
-LEAD = 2
-GRP = 2
+UNITS = [(0, 2, 1, 0, 1, 0), (2, 2, 1, 1, 1, 0), (4, 2, 2, 0, 2, 4), (6, 2, 2, 0, 2, 4)]
+WPOS = 2
 NU = len(UNITS)
 KMAX = max(u[2] for u in UNITS)
 
@@ -13,7 +11,7 @@ SCRATCH = {
     "xs": ("sbuf", [128, MB * TK], "bfloat16"),
     "rin": ("sbuf", [128, MB * TK], "bfloat16"),
     "wb": ("sbuf", [128, 2 * NL * 128], "bfloat16"),
-    "zero": ("sbuf", [128, SUB * TK], "float32"),
+    "zero": ("sbuf", [128, max(u[4] for u in UNITS) * TK], "float32"),
     "wst": ("dram", [2, 128, 128], "bfloat16"),
 }
 for _j in range(NL):
@@ -56,8 +54,8 @@ def _uniq(seq):
 
 
 def _pieces(u):
-    m0, nm = UNITS[u][0], UNITS[u][1]
-    return [(m, min(SUB, m0 + nm - m)) for m in range(m0, m0 + nm, SUB)]
+    m0, nm, sub = UNITS[u][0], UNITS[u][1], UNITS[u][4]
+    return [(m, min(sub, m0 + nm - m)) for m in range(m0, m0 + nm, sub)]
 
 
 def _plan(T, topo):
@@ -113,14 +111,8 @@ def _plan(T, topo):
 
 
 def _in_order(us):
-    seq = [(UNITS[u][2], u, p) for u in us[:LEAD] for p in _pieces(u)]
-    for g0 in range(0, len(us), GRP):
-        for j in range(NL):
-            for u in us[g0:g0 + GRP]:
-                for p in _pieces(u):
-                    if j >= UNITS[u][2] and (j, u, p) not in seq:
-                        seq.append((j, u, p))
-    return seq
+    seq = [(j + UNITS[u][5], u, p, j) for u in us for j in range(UNITS[u][2], NL) for p in _pieces(u)]
+    return [(j, u, p) for _, u, p, j in sorted(seq)]
 
 
 def rank_program(g, core, T, topo):
@@ -169,12 +161,12 @@ def rank_program(g, core, T, topo):
     if outs:
         for m in range(MB):
             load(T.xs[:, m * TK:(m + 1) * TK], T.x[m], sem["lx%d" % m])
+            if m == 3:
+                for st in staged:
+                    load(T.wst[st], wt[st][:], sem["stg%d" % st])
     for pr, j, st in mine_local:
         if st != so:
             load(slot(st, j), wt[st][:], wsem(st, j))
-    if outs:
-        for st in staged:
-            load(T.wst[st], wt[st][:], sem["stg%d" % st])
 
     tasks = []
     if outs:
@@ -244,11 +236,12 @@ def rank_program(g, core, T, topo):
         send_weights()
     else:
         for u in range(NU):
+            if u == WPOS:
+                send_weights()
             lo, hi = ucols(u)
             k = UNITS[u][2]
             g.wait_ge(sem.dv, done(so, k - 1, u))
             write(S[so]["work"][u], T.rin[:, lo:hi], T["a%d" % (k - 1)][:, lo:hi], sem["ar%d" % u])
-        send_weights()
     if core in P["relay"]:
         jobs = sorted(P["relay"][core])
         holder = [h for h in P["hand"] if (core, jobs[0][2]) in P["hand"][h]][0]
@@ -267,17 +260,17 @@ def rank_program(g, core, T, topo):
 
     if ins and core == S[si]["dst"]:
         res = T.y if si == 0 else T.z
-        jobs = [(idx[t] + 1, t[2], m) for t in tasks if t[0] == si and t[1] == NL - 1 for m in range(t[3][0], t[3][0] + t[3][1])]
-        jobs += [(None, u, m) for u in range(NU) if u not in mine for m in range(UNITS[u][0], UNITS[u][0] + UNITS[u][1])]
-        for v, u, m in jobs:
-            q = nq[0] % 2
-            nq[0] += 1
-            if v is not None:
-                queues[q].wait_ge(sem.dv, v)
-            else:
-                queues[q].wait_ge(sem["fn%d" % u], _count(topo.mask(S[si]["work"][u], core)))
-            queues[q].dma_start(res[m], last[:, m * TK:(m + 1) * TK]).then_inc(sem["sq%d" % q], 16)
-            stores[q] += 16
+        for u in range(NU):
+            for m0, nm in _pieces(u):
+                for m in range(m0, m0 + nm):
+                    q = nq[0] % 2
+                    nq[0] += 1
+                    if u in mine:
+                        queues[q].wait_ge(sem.dv, idx[(si, NL - 1, u, (m0, nm))] + 1)
+                    else:
+                        queues[q].wait_ge(sem["fn%d" % u], _count(topo.mask(S[si]["work"][u], core)))
+                    queues[q].dma_start(res[m], last[:, m * TK:(m + 1) * TK]).then_inc(sem["sq%d" % q], 16)
+                    stores[q] += 16
         for q in range(2):
             if stores[q]:
                 queues[q].wait_ge(sem["sq%d" % q], stores[q])

from concourse.bass import DstId, RemoteDMATransfer
from concourse.mybir import AluOpType

NL, MB, TK = 6, 8, 128
UNITS = [(0, 2, 1, 0, 1, 0), (2, 2, 1, 1, 1, 0), (4, 2, 2, 0, 2, 4), (6, 2, 2, 0, 2, 4)]
WPOS = 2
NU = len(UNITS)
KMAX = max(u[2] for u in UNITS)

SCRATCH = {
    "xs": ("sbuf", [128, MB * TK], "bfloat16"),
    "rin": ("sbuf", [128, MB * TK], "bfloat16"),
    "wb": ("sbuf", [128, 2 * NL * 128], "bfloat16"),
    "zero": ("sbuf", [128, max(u[4] for u in UNITS) * TK], "float32"),
    "wst": ("dram", [2, 128, 128], "bfloat16"),
}
for _j in range(NL):
    SCRATCH["a%d" % _j] = ("sbuf", [128, MB * TK], "bfloat16")
for _b in range(8):
    SCRATCH["ps%d" % _b] = ("psum", [128, 512], "float32")

SEMAPHORES = (["pe", "dv", "zs", "sent", "sq0", "sq1", "stg0", "stg1", "rl0", "rl1"]
              + ["ws%d" % s for s in range(2 * NL)] + ["lx%d" % m for m in range(MB)]
              + ["ar%d" % c for c in range(NU)] + ["fn%d" % c for c in range(NU)])


def _engines(mask):
    return [b for b in range(mask.bit_length()) if (mask >> b) & 1]


def _count(mask):
    return len(_engines(mask))


def _part(mask, parts, k):
    e = _engines(mask)
    n = len(e) // parts
    return sum(1 << b for b in e[k * n:(k + 1) * n])


def _pow2(n):
    p = 1
    while p < n:
        p *= 2
    return p


def _uniq(seq):
    out = []
    for v in seq:
        if v not in out:
            out.append(v)
    return out


def _pieces(u):
    m0, nm, sub = UNITS[u][0], UNITS[u][1], UNITS[u][4]
    return [(m, min(sub, m0 + nm - m)) for m in range(m0, m0 + nm, sub)]


def _plan(T, topo):
    cores = list(T.cores)
    world = range(2 * topo.CORES_PER_HOST)

    def neighbours(c):
        n = [d for d in world if d not in cores and topo.host(d) == topo.host(c) and topo.chip(d) == topo.chip(c)]
        return [d for d in n if topo.die(d) == topo.die(c)], [d for d in n if topo.die(d) != topo.die(c)]

    S = []
    for st in range(2):
        line = cores if st == 0 else cores[::-1]
        same, other = neighbours(line[-1])
        near = same + other
        S.append({"line": line, "src": line[0], "dst": line[-1],
                  "work": [line[-1] if u[3] == 0 else near[u[3] - 1] for u in UNITS]})
    local, direct, hand, relay, wexp = {}, {}, {}, {}, {}
    for h in cores:
        hops = []
        for st in range(2):
            j = S[st]["line"].index(h)
            want = []
            if j < KMAX:
                want.append((j - 0.5, S[st]["src"]))
            for u in range(NU):
                e = (j + (0.25 if UNITS[u][3] else 0), S[st]["work"][u])
                if j >= UNITS[u][2] and e not in want:
                    want.append(e)
            for pr, d in want:
                if d == h:
                    local.setdefault(h, []).append((pr, j, st))
                    wexp[(d, st, j)] = 16
                elif topo.may_write(h, d):
                    direct.setdefault(h, []).append((pr, j, st, d))
                    wexp[(d, st, j)] = _count(topo.mask(h, d))
                else:
                    hops.append((pr, j, st, d))
        if hops:
            same, other = neighbours(h)
            same = [c for c in same if all(topo.may_write(c, e[3]) for e in hops)]
            other = [c for c in other if all(topo.may_write(c, e[3]) for e in hops)]
            ring = []
            for i in range(max(len(same), len(other))):
                ring += other[i:i + 1] + same[i:i + 1]
            for i, (pr, j, st, d) in enumerate(sorted(hops)):
                r = ring[i % len(ring)]
                relay.setdefault(r, []).append((pr, j, st, d))
                wexp[(d, st, j)] = _count(topo.mask(r, d))
                if (r, st) not in hand.setdefault(h, []):
                    hand[h].append((r, st))
    return {"S": S, "local": local, "direct": direct, "hand": hand, "relay": relay, "wexp": wexp}


def _in_order(us):
    seq = [(j + UNITS[u][5], u, p, j) for u in us for j in range(UNITS[u][2], NL) for p in _pieces(u)]
    return [(j, u, p) for _, u, p, j in sorted(seq)]


def rank_program(g, core, T, topo):
    P = _plan(T, topo)
    S, sem = P["S"], T.sem
    sent = [0]
    queues = [g.sync, g.scalar]
    nq = [0]
    stores = [0, 0]
    last = T["a%d" % (NL - 1)]

    def slot(st, j):
        return T.wb[:, (st * NL + j) * 128:(st * NL + j + 1) * 128]

    def wsem(st, j):
        return sem["ws%d" % (st * NL + j)]

    def ucols(u):
        return UNITS[u][0] * TK, (UNITS[u][0] + UNITS[u][1]) * TK

    def load(out, in_, s):
        queues[nq[0] % 2].dma_start(out, in_).then_inc(s, 16)
        nq[0] += 1

    def write(d, out, in_, rsem):
        rid, pid = topo.addr(d, core)
        m = topo.mask(core, d)
        g.remote_dma(out_ap=out, in_ap=in_, remote_sem=rsem, local_sem=sem.sent, pid=pid, routing_id=rid,
                     dma_engine_mask=m)
        sent[0] += _count(m)

    outs = [st for st in range(2) if S[st]["src"] == core]
    ins = [st for st in range(2) if core in S[st]["work"] or core == S[st]["dst"]]
    so = outs[0] if outs else None
    si = ins[0] if ins else None
    wt = [T.w, T.u] if T.rank_of(core) is not None else None

    mine_local = sorted(P["local"].get(core, []))
    staged = _uniq([e[2] for e in sorted(P["direct"].get(core, []))] + [st for _, st in P["hand"].get(core, [])])
    if not outs:
        for st in staged:
            load(T.wst[st], wt[st][:], sem["stg%d" % st])
    for pr, j, st in mine_local:
        if st == so:
            load(slot(st, j), wt[st][:], wsem(st, j))
    if outs:
        for m in range(MB):
            load(T.xs[:, m * TK:(m + 1) * TK], T.x[m], sem["lx%d" % m])
            if m == 3:
                for st in staged:
                    load(T.wst[st], wt[st][:], sem["stg%d" % st])
    for pr, j, st in mine_local:
        if st != so:
            load(slot(st, j), wt[st][:], wsem(st, j))

    tasks = []
    if outs:
        tasks += [(so, j, u, p) for u in range(NU) for j in range(UNITS[u][2]) for p in _pieces(u)]
    mine = [u for u in range(NU) if ins and S[si]["work"][u] == core]
    tasks += [(si,) + t for t in _in_order(mine)]
    idx = {t: i for i, t in enumerate(tasks)}

    have, dv_seen = [], 0
    for i, (st, j, u, (m0, nm)) in enumerate(tasks):
        lo, hi = m0 * TK, (m0 + nm) * TK
        if (st, j) not in have:
            g.tensor.wait_ge(wsem(st, j), P["wexp"][(core, st, j)])
            have.append((st, j))
        need = i - 7
        if j == 0:
            for m in range(m0, m0 + nm):
                g.tensor.wait_ge(sem["lx%d" % m], 16)
            a = T.xs
        elif st == si and j == UNITS[u][2]:
            if ("ar", u) not in have:
                g.tensor.wait_ge(sem["ar%d" % u], _count(topo.mask(S[si]["src"], core)))
                have.append(("ar", u))
            a = T.rin
        else:
            need = max(need, idx[(st, j - 1, u, (m0, nm))] + 1)
            a = T["a%d" % (j - 1)]
        if need > dv_seen:
            g.tensor.wait_ge(sem.dv, need)
            dv_seen = need
        g.tensor.matmul(T["ps%d" % (i % 8)][:, 0:hi - lo], slot(st, j), a[:, lo:hi], start=True, stop=True).then_inc(sem.pe, 1)
    if tasks:
        g.vector.memset(T.zero[:], 0.0).then_inc(sem.zs, 1)
        g.vector.wait_ge(sem.zs, 1)
    for i, (st, j, u, (m0, nm)) in enumerate(tasks):
        lo, hi = m0 * TK, (m0 + nm) * TK
        g.vector.wait_ge(sem.pe, i + 1)
        g.vector.tensor_tensor(out=T["a%d" % j][:, lo:hi], in0=T["ps%d" % (i % 8)][:, 0:hi - lo],
                               in1=T.zero[:, 0:hi - lo], op=AluOpType.max).then_inc(sem.dv, 1)

    def done(st, j, u):
        return max(idx[(st, j, u, p)] for p in _pieces(u)) + 1

    def send_weights():
        got = []
        for pr, j, st, d in sorted(P["direct"].get(core, [])):
            if st not in got:
                g.wait_ge(sem["stg%d" % st], 16)
                got.append(st)
            write(d, slot(st, j), T.wst[st], wsem(st, j))
        hand = P["hand"].get(core, [])
        if hand:
            for st in _uniq([st for _, st in hand]):
                if st not in got:
                    g.wait_ge(sem["stg%d" % st], 16)
                    got.append(st)
            trs = []
            for k, (r, st) in enumerate(hand):
                rid, pid = topo.addr(r, core)
                m = _part(topo.mask(core, r), _pow2(len(hand)), k)
                trs.append(RemoteDMATransfer(dst_ids=[DstId(rid=rid, pnc=pid)], dma_engine_mask=m,
                                             remote_sem=sem["rl%d" % st], src=T.wst[st], dst=T.wst[st]))
                sent[0] += _count(m)
            g.remote_dma_fused(trs, local_sem=sem.sent)

    if not outs:
        send_weights()
    else:
        for u in range(NU):
            if u == WPOS:
                send_weights()
            lo, hi = ucols(u)
            k = UNITS[u][2]
            g.wait_ge(sem.dv, done(so, k - 1, u))
            write(S[so]["work"][u], T.rin[:, lo:hi], T["a%d" % (k - 1)][:, lo:hi], sem["ar%d" % u])
    if core in P["relay"]:
        jobs = sorted(P["relay"][core])
        holder = [h for h in P["hand"] if (core, jobs[0][2]) in P["hand"][h]][0]
        n_in = _count(_part(topo.mask(holder, core), _pow2(len(P["hand"][holder])), 0))
        got = []
        for pr, j, st, d in jobs:
            if st not in got:
                g.wait_ge(sem["rl%d" % st], n_in)
                got.append(st)
            write(d, slot(st, j), T.wst[st], wsem(st, j))
    if ins and core != S[si]["dst"]:
        for u in mine:
            lo, hi = ucols(u)
            g.wait_ge(sem.dv, done(si, NL - 1, u))
            write(S[si]["dst"], last[:, lo:hi], last[:, lo:hi], sem["fn%d" % u])

    if ins and core == S[si]["dst"]:
        res = T.y if si == 0 else T.z
        for u in range(NU):
            for m0, nm in _pieces(u):
                for m in range(m0, m0 + nm):
                    q = nq[0] % 2
                    nq[0] += 1
                    if u in mine:
                        queues[q].wait_ge(sem.dv, idx[(si, NL - 1, u, (m0, nm))] + 1)
                    else:
                        queues[q].wait_ge(sem["fn%d" % u], _count(topo.mask(S[si]["work"][u], core)))
                    queues[q].dma_start(res[m], last[:, m * TK:(m + 1) * TK]).then_inc(sem["sq%d" % q], 16)
                    stores[q] += 16
        for q in range(2):
            if stores[q]:
                queues[q].wait_ge(sem["sq%d" % q], stores[q])

    if tasks:
        g.wait_ge(sem.dv, len(tasks))
    if sent[0]:
        g.wait_ge(sem.sent, sent[0])
